import numpy as np
CORES = [66,74,82,90,194,202,210,218]
N = 8
def setup_inputs(rng):
    return {"x": rng.standard_normal((N, 128, N * 128), dtype=np.float32)}
def setup_inputs_big(rng):
    d = setup_inputs(rng)
    for k in ("x",): d[k] = (d[k].astype(np.float32) * 1048576.0).astype(d[k].dtype)
    return d
def setup_inputs_small(rng):
    d = setup_inputs(rng)
    for k in ("x",): d[k] = (d[k].astype(np.float32) * (1 / 1048576.0)).astype(d[k].dtype)
    return d
def setup_inputs_apart(rng):
    d = setup_inputs(rng)
    f = (10.0 ** rng.permutation(np.linspace(-1.5, 1.5, N))).astype(np.float32).reshape(N, 1, 1)
    for k in ("x",): d[k] = (d[k].astype(np.float32) * f).astype(d[k].dtype)
    return d
def reference(x):
    X = np.concatenate(list(x), axis=0)
    return {"y": np.stack([X.T[128 * r:128 * r + 128] for r in range(N)])}

from concourse.bass import DstId, RemoteDMATransfer
from concourse.mybir import AluOpType

BLK = 128
NR = 8
ORDER = (1, 2, 3, 0)
RAW = (True, False, False, False)
VIA = (False, False, False, False)

N_RAW = 2 * sum(1 for k in range(4) if RAW[k] and ORDER[k]) + sum(1 for k in range(4) if RAW[k] and not ORDER[k])
N_PRE = NR - 1 - N_RAW
N_VIA = sum(1 for v in VIA if v)

SCRATCH = {
    "xin": ("sbuf", [128, NR * BLK], "float32"),
    "snd": ("sbuf", [128, N_PRE * BLK], "float32"),
    "land": ("sbuf", [128, N_RAW * BLK], "float32"),
    "yout": ("sbuf", [128, NR * BLK], "float32"),
    "ones": ("sbuf", [128, BLK], "float32"),
    "ident": ("sbuf", [128, BLK], "float32"),
}
for _j in range(NR):
    SCRATCH["ps%d" % _j] = ("psum", [128, 512], "float32")
if N_VIA:
    SCRATCH["hbuf"] = ("sbuf", [128, N_VIA * BLK], "float32")

SEMAPHORES = (["fill", "idn", "sent", "st"] + ["ld%d" % k for k in range(4)] + ["a%d" % s for s in range(NR)]
              + ["pe%d" % j for j in range(NR)] + ["cp%d" % j for j in range(NR)] + ["h%d" % k for k in range(N_VIA)])


def _bits(m):
    return [i for i in range(m.bit_length()) if (m >> i) & 1]


def _mask(engs):
    m = 0
    for e in engs:
        m |= 1 << e
    return m


def _cols(j):
    return slice(j * BLK, (j + 1) * BLK)


def _runs(blocks):
    out = []
    for b in sorted(blocks):
        if out and out[-1][1] == b:
            out[-1][1] = b + 1
        else:
            out.append([b, b + 1])
    return out


def _pairs(cores, topo):
    pairs, seen = [], []
    for a in range(len(cores)):
        if a not in seen:
            grp = [a] + [b for b in range(len(cores)) if b != a and topo.mates(cores[a], cores[b])]
            seen.extend(grp)
            pairs.append(grp)
    return pairs


def _helper(r, cores, topo):
    me, n = cores[r], topo.CORES_PER_CHIP
    for c in range(max(0, me - n + 1), me + n):
        if (c != me and topo.host(c) == topo.host(me) and topo.chip(c) == topo.chip(me) and topo.die(c) != topo.die(me)
                and all(topo.may_write(c, d) for d in cores)):
            return c
    return None


def _plan(r, cores, topo):
    pairs = _pairs(cores, topo)
    p = [i for i, grp in enumerate(pairs) if r in grp][0]
    me, calls, pre, via = cores[r], [], 0, 0
    for k in range(4):
        grp = pairs[p ^ ORDER[k]]
        dests = sorted((d for d in grp if d != r), key=lambda d: 0 if topo.same_plane(me, cores[d]) else 1)
        far = [d for d in dests if VIA[k] and not topo.same_plane(me, cores[d]) and not topo.mates(me, cores[d])]
        near = [d for d in dests if d not in far]
        off = _bits(topo.mask(me, cores[dests[0]]))
        items = []
        for i, d in enumerate(near):
            n = len(off) // len(near)
            items.append(dict(dst=d, via=None, mask=_mask(off[i * n:(i + 1) * n]), count=n))
        for d in far:
            h = _helper(r, cores, topo)
            on = [e for e in _bits(topo.mask(me, h)) if e not in off]
            fwd = topo.mask(h, cores[d])
            items.append(dict(dst=d, via=h, mask=_mask(on), hcount=len(on), fwd=fwd, count=len(_bits(fwd)), hslot=via))
            via += 1
        for it in items:
            if not RAW[k]:
                it["slot"] = pre
                pre += 1
        calls.append((grp, RAW[k], items))
    return calls


def _incoming(me, cores, topo):
    inc = {}
    for s in range(len(cores)):
        if s != me:
            for k, (grp, raw, items) in enumerate(_plan(s, cores, topo)):
                for it in items:
                    if it["dst"] == me:
                        inc[s] = [k, raw, it["count"], None]
    for i, s in enumerate(sorted(s for s in inc if inc[s][1])):
        inc[s][3] = i
    return inc


def _landing(T, s, d, cores, topo):
    k, raw, count, slot = _incoming(d, cores, topo)[s]
    return T.land[:, _cols(slot)] if raw else T.yout[:, _cols(s)]


def _forwarder(g, core, T, topo):
    cores = T.cores
    for r in range(len(cores)):
        total = 0
        for grp, raw, items in _plan(r, cores, topo):
            for it in items:
                if it["via"] == core:
                    rid, pid = topo.addr(cores[it["dst"]], core)
                    g.wait_ge(T.sem["h%d" % it["hslot"]], it["hcount"])
                    g.remote_dma(_landing(T, r, it["dst"], cores, topo), T.hbuf[:, _cols(it["hslot"])],
                                 T.sem["a%d" % r], T.sem.sent, pid, rid, it["fwd"])
                    total += it["count"]
        if total:
            g.wait_ge(T.sem.sent, total)


def rank_program(g, core, T, topo):
    rank = T.rank_of(core)
    if rank is None:
        if N_VIA:
            _forwarder(g, core, T, topo)
        return
    cores = T.cores
    calls = _plan(rank, cores, topo)
    inc = _incoming(rank, cores, topo)
    dmaq = (g.sync, g.scalar)

    nld = []
    for k, (grp, raw, items) in enumerate(calls):
        runs = _runs(grp)
        for a, b in runs:
            c = slice(a * BLK, b * BLK)
            dmaq[k % 2].dma_start(T.xin[:, c], T.x[:, c]).then_inc(T.sem["ld%d" % k], 16)
        nld.append(16 * len(runs))

    g.vector.memset(T.ones[:], 1.0).then_inc(T.sem.fill, 1)
    g.wait_ge(T.sem.fill, 1)
    g.affine_select(T.ident[:], T.ones[:], [[-1, BLK]], AluOpType.is_equal, 0.0, 0, 1).then_inc(T.sem.idn, 1)
    g.tensor.wait_ge(T.sem.idn, 1)

    jobs = []
    for k, (grp, raw, items) in enumerate(calls):
        if not raw:
            for it in items:
                it["job"] = len(jobs)
                jobs.append((T.xin[:, _cols(it["dst"])], T.sem["ld%d" % k], nld[k], T.snd[:, _cols(it["slot"])]))
    kown = [k for k in range(4) if rank in calls[k][0]][0]
    done = {rank: len(jobs)}
    jobs.append((T.xin[:, _cols(rank)], T.sem["ld%d" % kown], nld[kown], T.yout[:, _cols(rank)]))
    for s in sorted(inc, key=lambda s: inc[s][0]):
        if inc[s][1]:
            done[s] = len(jobs)
            jobs.append((T.land[:, _cols(inc[s][3])], T.sem["a%d" % s], inc[s][2], T.yout[:, _cols(s)]))
    for j, (src, sem, val, dst) in enumerate(jobs):
        bank = T["ps%d" % j][:, 0:BLK]
        g.tensor.wait_ge(sem, val)
        g.tensor.transpose(bank, src, T.ident[:]).then_inc(T.sem["pe%d" % j], 1)
        g.vector.wait_ge(T.sem["pe%d" % j], 1)
        g.vector.tensor_copy(dst, bank).then_inc(T.sem["cp%d" % j], 1)

    sent = 0
    for k, (grp, raw, items) in enumerate(calls):
        trs = []
        if raw:
            g.wait_ge(T.sem["ld%d" % k], nld[k])
        for it in items:
            if raw:
                src = T.xin[:, _cols(it["dst"])]
            else:
                g.wait_ge(T.sem["cp%d" % it["job"]], 1)
                src = T.snd[:, _cols(it["slot"])]
            if it["via"] is None:
                rid, pid = topo.addr(cores[it["dst"]], core)
                trs.append((_landing(T, rank, it["dst"], cores, topo), src, T.sem["a%d" % rank], pid, rid, it["mask"]))
            else:
                rid, pid = topo.addr(it["via"], core)
                trs.append((T.hbuf[:, _cols(it["hslot"])], src, T.sem["h%d" % it["hslot"]], pid, rid, it["mask"]))
            sent += len(_bits(it["mask"]))
        if len(trs) == 1:
            dst, src, sem, pid, rid, m = trs[0]
            g.remote_dma(dst, src, sem, T.sem.sent, pid, rid, m)
        else:
            g.remote_dma_fused([RemoteDMATransfer(dst_ids=[DstId(rid=rid, pnc=pid)], dma_engine_mask=m, remote_sem=sem,
                                                  src=src, dst=dst) for dst, src, sem, pid, rid, m in trs],
                               local_sem=T.sem.sent)

    nst = 0
    for k, (grp, raw, items) in enumerate(calls):
        q = dmaq[(k + 1) % 2]
        for s in grp:
            if s in done:
                q.wait_ge(T.sem["cp%d" % done[s]], 1)
            else:
                q.wait_ge(T.sem["a%d" % s], inc[s][2])
        for a, b in _runs(grp):
            c = slice(a * BLK, b * BLK)
            q.dma_start(T.y[:, c], T.yout[:, c]).then_inc(T.sem.st, 16)
            nst += 16
    g.wait_ge(T.sem.sent, sent)
    g.wait_ge(T.sem.st, nst)
